import numpy as np, ml_dtypes
CORES = [44,45,46,47,172,173,174,175,300,301,302,303,428,429,430,431]
N = 16
TK = 512
def setup_inputs(rng):
    return {"c": rng.standard_normal((N, 128, 128), dtype=np.float32).astype(ml_dtypes.bfloat16), "x": rng.standard_normal((N, 128, TK), dtype=np.float32).astype(ml_dtypes.bfloat16)}
def setup_inputs_big(rng):
    d = setup_inputs(rng)
    for k in ("c", "x"): d[k] = (d[k].astype(np.float32) * 1024.0).astype(d[k].dtype)
    return d
def setup_inputs_small(rng):
    d = setup_inputs(rng)
    for k in ("c", "x"): d[k] = (d[k].astype(np.float32) * (1 / 1024.0)).astype(d[k].dtype)
    return d
def setup_inputs_apart(rng):
    d = setup_inputs(rng)
    f = (10.0 ** rng.permutation(np.linspace(-1.5, 1.5, N))).astype(np.float32).reshape(N, 1, 1)
    for k in ("c", "x"): d[k] = (d[k].astype(np.float32) * f).astype(d[k].dtype)
    return d
def reference(c, x):
    C, X = c.astype(np.float64), x.astype(np.float64)
    y = np.zeros((N, 128, TK))
    for r in range(N):
        for j in range(N):
            y[r] += C[(r - j) % N].T @ X[j]
    return {"y": y.astype(ml_dtypes.bfloat16 if x.dtype != np.float64 else np.float64)}

@@ -1,0 +1,188 @@
+from concourse.bass import DstId, RemoteDMATransfer
+from concourse.mybir import AluOpType
+
+CW, XW = 128, 512
+SW = CW + XW
+
+SCRATCH = {
+    "own": ("sbuf", [128, CW + XW + CW], "bfloat16"),
+    "rx": ("sbuf", [128, 2 * SW], "bfloat16"),
+    "dg": ("sbuf", [128, SW], "bfloat16"),
+    "cp": ("sbuf", [128, 4 * 4 * CW], "bfloat16"),
+    "pb": ("sbuf", [128, 3 * XW], "bfloat16"),
+    "pr": ("sbuf", [128, 4 * XW], "bfloat16"),
+    "ysb": ("sbuf", [128, XW], "bfloat16"),
+    "acc0": ("psum", [128, XW], "float32"),
+    "acc1": ("psum", [128, XW], "float32"),
+    "acc2": ("psum", [128, XW], "float32"),
+    "acc3": ("psum", [128, XW], "float32"),
+    "t1": ("psum", [128, XW], "float32"),
+    "t2": ("psum", [128, XW], "float32"),
+}
+SEMAPHORES = (["ldx", "ldc", "arrA", "arrB", "arrD", "sent", "va", "st"]
+              + ["cpo%d" % p for p in range(4)] + ["cpp%d" % p for p in range(4)] + ["cpd%d" % p for p in range(4)]
+              + ["pra%d" % p for p in range(4)] + ["mm%d" % i for i in range(4)] + ["ev%d" % i for i in range(3)])
+
+
+def _bits(mask):
+    return bin(mask).count("1")
+
+
+def _ring(T, topo):
+    cores = list(T.cores)
+    hosts = []
+    for c in cores:
+        if topo.host(c) not in hosts:
+            hosts.append(topo.host(c))
+    members = {h: [r for r, c in enumerate(cores) if topo.host(c) == h] for h in hosts}
+    first = hosts[0]
+    near = [h for h in hosts[1:] if topo.may_write(cores[members[first][0]], cores[members[h][0]])]
+    far = [h for h in hosts[1:] if h not in near]
+    return [first, near[0], far[0], near[1]], members
+
+
+def rank_program(g, core, T, topo):
+    me = T.rank_of(core)
+    if me is None:
+        return
+    cores = list(T.cores)
+    n = len(cores)
+    ring, members = _ring(T, topo)
+    h = topo.host(core)
+    l = members[h].index(me)
+    pos = ring.index(h)
+    nxt, prv, dia = ring[(pos + 1) % 4], ring[(pos - 1) % 4], ring[(pos + 2) % 4]
+    rel = {h: "own", prv: "A", nxt: "B", dia: "D"}
+    even = l % 2 == 0
+    S = T.sem
+    peers = [q for q in range(4) if q != l]
+
+    c_nxt, c_prv = cores[members[nxt][l]], cores[members[prv][l]]
+    m_off = topo.mask(core, c_nxt) & topo.mask(core, c_prv)
+    m_on = topo.mask(core, cores[members[h][peers[0]]])
+    m_up = m_on & ~m_off
+    if _bits(m_up) not in (1, 2, 4, 8, 16):
+        m_up = m_on
+    n_off, n_on, n_up = _bits(m_off), _bits(m_on), _bits(m_up)
+    sent = [0]
+
+    def send(dst, out_ap, in_ap, sem, mask):
+        rid, pid = topo.addr(dst, core)
+        g.remote_dma(out_ap=out_ap, in_ap=in_ap, remote_sem=sem, local_sem=S.sent, pid=pid, routing_id=rid,
+                     dma_engine_mask=mask)
+        sent[0] += _bits(mask)
+
+    def to_peers(lo, hi, in_ap, semname, mask):
+        ids = [topo.addr(cores[members[h][q]], core) for q in peers]
+        out = T.cp[:, l * 4 * CW + lo:l * 4 * CW + hi]
+        g.remote_dma_fused([RemoteDMATransfer(dst_ids=[DstId(rid=a[0], pnc=a[1]) for a in ids], dma_engine_mask=mask,
+                                              remote_sem=S["%s%d" % (semname, l)], srcs=[in_ap],
+                                              dsts=[out for a in ids], alu_op=0)], local_sem=S.sent)
+        sent[0] += _bits(mask)
+
+    g.scalar.dma_start(T.own[:, 0:CW], T.c[:, :]).then_inc(S.ldc, 16)
+    g.scalar.dma_start(T.own[:, CW + XW:CW + XW + CW], T.c[:, :]).then_inc(S.ldc, 16)
+    g.sync.dma_start(T.own[:, CW:CW + XW], T.x[:, :]).then_inc(S.ldx, 16)
+
+    g.wait_ge(S.ldc, 32)
+    g.wait_ge(S.ldx, 16)
+
+    def send_next():
+        send(c_nxt, T.rx[:, 0:SW], T.own[:, CW:CW + SW], S.arrA, m_off)
+
+    def send_prev():
+        send(c_prv, T.rx[:, SW:2 * SW], T.own[:, 0:SW], S.arrB, m_off)
+
+    if even:
+        send_next()
+        send_prev()
+    else:
+        send_prev()
+        send_next()
+    to_peers(0, CW, T.own[:, 0:CW], "cpo", m_up)
+    if even:
+        g.wait_ge(S.arrA, n_off)
+        send(c_nxt, T.dg[:, :], T.rx[:, 0:SW], S.arrD, m_off)
+        g.wait_ge(S.arrB, n_off)
+    else:
+        g.wait_ge(S.arrB, n_off)
+        send(c_prv, T.dg[:, :], T.rx[:, SW:2 * SW], S.arrD, m_off)
+        g.wait_ge(S.arrA, n_off)
+    to_peers(CW, 3 * CW, T.rx[:, XW:XW + 2 * CW], "cpp", m_up)
+    g.wait_ge(S.arrD, n_off)
+    to_peers(3 * CW, 4 * CW, T.dg[:, XW:SW] if even else T.dg[:, 0:CW], "cpd", m_on)
+
+    t_a, t_b = (3.0, 4.0) if even else (4.0, 3.0)
+
+    def xloc(j):
+        r_ = rel[topo.host(cores[j])]
+        if r_ == "own":
+            return T.own[:, CW:CW + XW], ("ldx", 16), 0.0
+        if r_ == "A":
+            return T.rx[:, 0:XW], ("arrA", n_off), t_a
+        if r_ == "B":
+            return T.rx[:, SW + CW:2 * SW], ("arrB", n_off), t_b
+        return (T.dg[:, 0:XW] if even else T.dg[:, CW:SW]), ("arrD", n_off), 6.5
+
+    def cloc(k):
+        hk = topo.host(cores[k])
+        q, r_ = members[hk].index(k), rel[hk]
+        if q == l:
+            if r_ == "own":
+                return T.own[:, 0:CW], ("ldc", 32), 0.0
+            if r_ == "A":
+                return T.rx[:, XW:SW], ("arrA", n_off), t_a
+            if r_ == "B":
+                return T.rx[:, SW:SW + CW], ("arrB", n_off), t_b
+            return (T.dg[:, XW:SW] if even else T.dg[:, 0:CW]), ("arrD", n_off), 6.5
+        b = q * 4 * CW
+        if r_ == "own":
+            return T.cp[:, b:b + CW], ("cpo%d" % q, n_up), 4.5
+        if r_ == "A":
+            return T.cp[:, b + CW:b + 2 * CW], ("cpp%d" % q, n_up), 7.0
+        if r_ == "B":
+            return T.cp[:, b + 2 * CW:b + 3 * CW], ("cpp%d" % q, n_up), 7.0
+        return T.cp[:, b + 3 * CW:b + 4 * CW], ("cpd%d" % q, n_on), 9.5
+
+    prods = []
+    for hh in ring:
+        j = members[hh][l]
+        for d in range(4):
+            r = members[h][d]
+            xa, xs, xt = xloc(j)
+            ca, cs, ct = cloc((r - j) % n)
+            prods.append((max(xt, ct), 1 if d == l else 0, d, xa, xs, ca, cs))
+    prods.sort(key=lambda t: (t[0], t[1], t[2]))
+
+    acc = [T.acc0, T.acc1, T.acc2, T.acc3]
+    seen, done, order = set(), [0, 0, 0, 0], []
+    for (_, _, d, xa, xs, ca, cs) in prods:
+        for sm in (xs, cs):
+            if sm not in seen:
+                seen.add(sm)
+                g.tensor.wait_ge(S[sm[0]], sm[1])
+        done[d] += 1
+        mmi = g.tensor.matmul(out=acc[d][:, :], lhsT=ca, rhs=xa, start=done[d] == 1, stop=done[d] == 4)
+        if done[d] == 4:
+            mmi.then_inc(S["mm%d" % d], 1)
+            if d != l:
+                order.append(d)
+
+    for i, d in enumerate(order):
+        g.vector.wait_ge(S["mm%d" % d], 1)
+        g.vector.tensor_copy(out=T.pb[:, i * XW:(i + 1) * XW], in_=acc[d][:, :]).then_inc(S["ev%d" % i], 1)
+        g.wait_ge(S["ev%d" % i], 1)
+        send(cores[members[h][d]], T.pr[:, l * XW:(l + 1) * XW], T.pb[:, i * XW:(i + 1) * XW], S["pra%d" % l], m_on)
+
+    g.vector.wait_ge(S["mm%d" % l], 1)
+    chain = [acc[l][:, :], T.t1[:, :], T.t2[:, :], T.ysb[:, :]]
+    for i, q in enumerate(peers):
+        g.vector.wait_ge(S["pra%d" % q], n_on)
+        if i:
+            g.vector.wait_ge(S.va, i)
+        g.vector.tensor_tensor(out=chain[i + 1], in0=chain[i], in1=T.pr[:, q * XW:(q + 1) * XW],
+                               op=AluOpType.add).then_inc(S.va, 1)
+    g.sync.wait_ge(S.va, 3)
+    g.sync.dma_start(T.y[:, :], T.ysb[:, :]).then_inc(S.st, 16)
+    g.wait_ge(S.sent, sent[0])
+    g.wait_ge(S.st, 16)

@@ -8,19 +8,22 @@ SCRATCH = {
     "own": ("sbuf", [128, CW + XW + CW], "bfloat16"),
     "rx": ("sbuf", [128, 2 * SW], "bfloat16"),
     "dg": ("sbuf", [128, SW], "bfloat16"),
-    "cp": ("sbuf", [128, 4 * 4 * CW], "bfloat16"),
+    "cp": ("sbuf", [128, 4 * 3 * CW], "bfloat16"),
+    "fs": ("sbuf", [128, 4 * SW], "bfloat16"),
+    "xe": ("sbuf", [128, 4 * XW], "bfloat16"),
     "pb": ("sbuf", [128, 3 * XW], "bfloat16"),
     "pr": ("sbuf", [128, 4 * XW], "bfloat16"),
+    "e1": ("sbuf", [128, XW], "float32"),
     "ysb": ("sbuf", [128, XW], "bfloat16"),
     "acc0": ("psum", [128, XW], "float32"),
     "acc1": ("psum", [128, XW], "float32"),
     "acc2": ("psum", [128, XW], "float32"),
     "acc3": ("psum", [128, XW], "float32"),
     "t1": ("psum", [128, XW], "float32"),
-    "t2": ("psum", [128, XW], "float32"),
 }
-SEMAPHORES = (["ldx", "ldc", "arrA", "arrB", "arrD", "sent", "va", "st"]
-              + ["cpo%d" % p for p in range(4)] + ["cpp%d" % p for p in range(4)] + ["cpd%d" % p for p in range(4)]
+SEMAPHORES = (["ldx", "ldc1", "ldc2", "arrA", "arrB", "arrD", "sent", "va", "st"]
+              + ["cpo%d" % p for p in range(4)] + ["cpp%d" % p for p in range(4)] + ["fsa%d" % p for p in range(4)]
+              + ["xea%d" % p for p in range(4)]
               + ["pra%d" % p for p in range(4)] + ["mm%d" % i for i in range(4)] + ["ev%d" % i for i in range(3)])
 
 
@@ -57,6 +60,23 @@ def rank_program(g, core, T, topo):
     S = T.sem
     peers = [q for q in range(4) if q != l]
 
+    def rl(r):
+        return rel[topo.host(cores[r])]
+
+    def col(r):
+        return members[topo.host(cores[r])].index(r)
+
+    def prods_of(lp):
+        out = []
+        for d in range(4):
+            r = members[h][d]
+            for j in range(n):
+                k = (r - j) % n
+                late = rl(j) == "D" or rl(k) == "D"
+                if (late and d == lp) or (not late and col(j) == lp):
+                    out.append((d, j, k))
+        return out
+
     c_nxt, c_prv = cores[members[nxt][l]], cores[members[prv][l]]
     m_off = topo.mask(core, c_nxt) & topo.mask(core, c_prv)
     m_on = topo.mask(core, cores[members[h][peers[0]]])
@@ -72,50 +92,24 @@ def rank_program(g, core, T, topo):
                      dma_engine_mask=mask)
         sent[0] += _bits(mask)
 
-    def to_peers(lo, hi, in_ap, semname, mask):
-        ids = [topo.addr(cores[members[h][q]], core) for q in peers]
-        out = T.cp[:, l * 4 * CW + lo:l * 4 * CW + hi]
+    def spread(cols, out_ap, in_ap, sem, mask):
+        ids = [topo.addr(cores[members[h][q]], core) for q in cols]
         g.remote_dma_fused([RemoteDMATransfer(dst_ids=[DstId(rid=a[0], pnc=a[1]) for a in ids], dma_engine_mask=mask,
-                                              remote_sem=S["%s%d" % (semname, l)], srcs=[in_ap],
-                                              dsts=[out for a in ids], alu_op=0)], local_sem=S.sent)
+                                              remote_sem=sem, srcs=[in_ap], dsts=[out_ap for a in ids], alu_op=0)],
+                           local_sem=S.sent)
         sent[0] += _bits(mask)
 
-    g.scalar.dma_start(T.own[:, 0:CW], T.c[:, :]).then_inc(S.ldc, 16)
-    g.scalar.dma_start(T.own[:, CW + XW:CW + XW + CW], T.c[:, :]).then_inc(S.ldc, 16)
-    g.sync.dma_start(T.own[:, CW:CW + XW], T.x[:, :]).then_inc(S.ldx, 16)
-
-    g.wait_ge(S.ldc, 32)
-    g.wait_ge(S.ldx, 16)
-
-    def send_next():
-        send(c_nxt, T.rx[:, 0:SW], T.own[:, CW:CW + SW], S.arrA, m_off)
-
-    def send_prev():
-        send(c_prv, T.rx[:, SW:2 * SW], T.own[:, 0:SW], S.arrB, m_off)
-
-    if even:
-        send_next()
-        send_prev()
-    else:
-        send_prev()
-        send_next()
-    to_peers(0, CW, T.own[:, 0:CW], "cpo", m_up)
-    if even:
-        g.wait_ge(S.arrA, n_off)
-        send(c_nxt, T.dg[:, :], T.rx[:, 0:SW], S.arrD, m_off)
-        g.wait_ge(S.arrB, n_off)
-    else:
-        g.wait_ge(S.arrB, n_off)
-        send(c_prv, T.dg[:, :], T.rx[:, SW:2 * SW], S.arrD, m_off)
-        g.wait_ge(S.arrA, n_off)
-    to_peers(CW, 3 * CW, T.rx[:, XW:XW + 2 * CW], "cpp", m_up)
-    g.wait_ge(S.arrD, n_off)
-    to_peers(3 * CW, 4 * CW, T.dg[:, XW:SW] if even else T.dg[:, 0:CW], "cpd", m_on)
-
+    c_lo, c_hi = T.own[:, 0:CW], T.own[:, CW + XW:CW + XW + CW]
+    c_1st, c_2nd = (c_hi, c_lo) if even else (c_lo, c_hi)
     t_a, t_b = (3.0, 4.0) if even else (4.0, 3.0)
 
     def xloc(j):
-        r_ = rel[topo.host(cores[j])]
+        r_, q = rl(j), col(j)
+        if q != l:
+            if r_ == "D":
+                b = q * SW + (0 if q % 2 == 0 else CW)
+                return T.fs[:, b:b + XW], ("fsa%d" % q, n_on), 9.5
+            return T.xe[:, q * XW:(q + 1) * XW], ("xea%d" % q, n_on), 8.0
         if r_ == "own":
             return T.own[:, CW:CW + XW], ("ldx", 16), 0.0
         if r_ == "A":
@@ -125,45 +119,106 @@ def rank_program(g, core, T, topo):
         return (T.dg[:, 0:XW] if even else T.dg[:, CW:SW]), ("arrD", n_off), 6.5
 
     def cloc(k):
-        hk = topo.host(cores[k])
-        q, r_ = members[hk].index(k), rel[hk]
+        r_, q = rl(k), col(k)
         if q == l:
             if r_ == "own":
-                return T.own[:, 0:CW], ("ldc", 32), 0.0
+                return c_1st, ("ldc1", 16), 0.0
             if r_ == "A":
                 return T.rx[:, XW:SW], ("arrA", n_off), t_a
             if r_ == "B":
                 return T.rx[:, SW:SW + CW], ("arrB", n_off), t_b
             return (T.dg[:, XW:SW] if even else T.dg[:, 0:CW]), ("arrD", n_off), 6.5
-        b = q * 4 * CW
+        if r_ == "D":
+            b = q * SW + (XW if q % 2 == 0 else 0)
+            return T.fs[:, b:b + CW], ("fsa%d" % q, n_on), 9.5
+        b = q * 3 * CW
         if r_ == "own":
             return T.cp[:, b:b + CW], ("cpo%d" % q, n_up), 4.5
         if r_ == "A":
-            return T.cp[:, b + CW:b + 2 * CW], ("cpp%d" % q, n_up), 7.0
-        if r_ == "B":
-            return T.cp[:, b + 2 * CW:b + 3 * CW], ("cpp%d" % q, n_up), 7.0
-        return T.cp[:, b + 3 * CW:b + 4 * CW], ("cpd%d" % q, n_on), 9.5
+            return T.cp[:, b + CW:b + 2 * CW], ("cpp%d" % q, n_on), 7.0
+        return T.cp[:, b + 2 * CW:b + 3 * CW], ("cpp%d" % q, n_on), 7.0
 
-    prods = []
-    for hh in ring:
-        j = members[hh][l]
-        for d in range(4):
-            r = members[h][d]
-            xa, xs, xt = xloc(j)
-            ca, cs, ct = cloc((r - j) % n)
-            prods.append((max(xt, ct), 1 if d == l else 0, d, xa, xs, ca, cs))
-    prods.sort(key=lambda t: (t[0], t[1], t[2]))
+    need_o, need_p, need_x = [], [], {}
+    for q in peers:
+        pq = prods_of(q)
+        ks = [k for (_, _, k) in pq if col(k) == l]
+        if any(rl(k) == "own" for k in ks):
+            need_o.append(q)
+        if any(rl(k) in ("A", "B") for k in ks):
+            need_p.append(q)
+        for (_, j, _) in pq:
+            if col(j) == l and rl(j) != "D" and q not in need_x.setdefault(j, []):
+                need_x[j].append(q)
+
+    g.sync.dma_start(T.own[:, CW:CW + XW], T.x[:, :]).then_inc(S.ldx, 16)
+    g.scalar.dma_start(c_1st, T.c[:, :]).then_inc(S.ldc1, 16)
+    g.scalar.dma_start(c_2nd, T.c[:, :]).then_inc(S.ldc2, 16)
+
+    def send_next():
+        send(c_nxt, T.rx[:, 0:SW], T.own[:, CW:CW + SW], S.arrA, m_off)
+
+    def send_prev():
+        send(c_prv, T.rx[:, SW:2 * SW], T.own[:, 0:SW], S.arrB, m_off)
+
+    def near_x(which):
+        for j in sorted(need_x):
+            if need_x[j] and (rl(j) == "own") == which:
+                spread(need_x[j], T.xe[:, l * XW:(l + 1) * XW], xloc(j)[0], S["xea%d" % l], m_on)
+
+    g.wait_ge(S.ldc1, 16)
+    g.wait_ge(S.ldx, 16)
+    if even:
+        send_next()
+        g.wait_ge(S.ldc2, 16)
+        send_prev()
+    else:
+        send_prev()
+        g.wait_ge(S.ldc2, 16)
+        send_next()
+    if need_o:
+        spread(need_o, T.cp[:, l * 3 * CW:l * 3 * CW + CW], c_1st, S["cpo%d" % l], m_up)
+    if even:
+        g.wait_ge(S.arrA, n_off)
+        send(c_nxt, T.dg[:, :], T.rx[:, 0:SW], S.arrD, m_off)
+    else:
+        g.wait_ge(S.arrB, n_off)
+        send(c_prv, T.dg[:, :], T.rx[:, SW:2 * SW], S.arrD, m_off)
+    g.wait_ge(S.arrB if even else S.arrA, n_off)
+    if need_p:
+        spread(need_p, T.cp[:, l * 3 * CW + CW:l * 3 * CW + 3 * CW], T.rx[:, XW:XW + 2 * CW], S["cpp%d" % l], m_on)
+    near_x(True)
+    near_x(False)
+    g.wait_ge(S.arrD, n_off)
+    spread(peers, T.fs[:, l * SW:(l + 1) * SW], T.dg[:, :], S["fsa%d" % l], m_on)
+
+    items = []
+    for (d, j, k) in prods_of(l):
+        xa, xs, xt = xloc(j)
+        ca, cs, ct = cloc(k)
+        items.append((max(xt, ct), (d - l - 1) % 4, d, xa, xs, ca, cs))
+    items.sort(key=lambda t: (t[0], t[1]))
+    mine = [t for t in items if t[2] == l]
+    oth = [t for t in items if t[2] != l]
+    last = {}
+    for t in oth:
+        last[t[2]] = t
+    tail = sorted(last.values(), key=lambda t: t[1])
+    oth = [t for t in oth if last[t[2]] is not t] + tail
+    seq = [t for t in mine if t[0] <= 4.5] + oth + [t for t in mine if t[0] > 4.5]
+    total = [0, 0, 0, 0]
+    for t in seq:
+        total[t[2]] += 1
 
     acc = [T.acc0, T.acc1, T.acc2, T.acc3]
     seen, done, order = set(), [0, 0, 0, 0], []
-    for (_, _, d, xa, xs, ca, cs) in prods:
+    for (_, _, d, xa, xs, ca, cs) in seq:
         for sm in (xs, cs):
             if sm not in seen:
                 seen.add(sm)
                 g.tensor.wait_ge(S[sm[0]], sm[1])
         done[d] += 1
-        mmi = g.tensor.matmul(out=acc[d][:, :], lhsT=ca, rhs=xa, start=done[d] == 1, stop=done[d] == 4)
-        if done[d] == 4:
+        mmi = g.tensor.matmul(out=acc[d][:, :], lhsT=ca, rhs=xa, start=done[d] == 1, stop=done[d] == total[d])
+        if done[d] == total[d]:
             mmi.then_inc(S["mm%d" % d], 1)
             if d != l:
                 order.append(d)
@@ -174,14 +229,18 @@ def rank_program(g, core, T, topo):
         g.wait_ge(S["ev%d" % i], 1)
         send(cores[members[h][d]], T.pr[:, l * XW:(l + 1) * XW], T.pb[:, i * XW:(i + 1) * XW], S["pra%d" % l], m_on)
 
+    q1, q2, q3 = (l - 1) % 4, (l - 2) % 4, (l - 3) % 4
+    g.vector.wait_ge(S["pra%d" % q1], n_on)
+    g.vector.wait_ge(S["pra%d" % q2], n_on)
+    g.vector.tensor_tensor(out=T.e1[:, :], in0=T.pr[:, q1 * XW:(q1 + 1) * XW], in1=T.pr[:, q2 * XW:(q2 + 1) * XW],
+                           op=AluOpType.add).then_inc(S.va, 1)
+    g.vector.wait_ge(S.va, 1)
     g.vector.wait_ge(S["mm%d" % l], 1)
-    chain = [acc[l][:, :], T.t1[:, :], T.t2[:, :], T.ysb[:, :]]
-    for i, q in enumerate(peers):
-        g.vector.wait_ge(S["pra%d" % q], n_on)
-        if i:
-            g.vector.wait_ge(S.va, i)
-        g.vector.tensor_tensor(out=chain[i + 1], in0=chain[i], in1=T.pr[:, q * XW:(q + 1) * XW],
-                               op=AluOpType.add).then_inc(S.va, 1)
+    g.vector.tensor_tensor(out=T.t1[:, :], in0=acc[l][:, :], in1=T.e1[:, :], op=AluOpType.add).then_inc(S.va, 1)
+    g.vector.wait_ge(S.va, 2)
+    g.vector.wait_ge(S["pra%d" % q3], n_on)
+    g.vector.tensor_tensor(out=T.ysb[:, :], in0=T.t1[:, :], in1=T.pr[:, q3 * XW:(q3 + 1) * XW],
+                           op=AluOpType.add).then_inc(S.va, 1)
     g.sync.wait_ge(S.va, 3)
     g.sync.dma_start(T.y[:, :], T.ysb[:, :]).then_inc(S.st, 16)
     g.wait_ge(S.sent, sent[0])

@@ -6,6 +6,7 @@ SW = CW + XW
 
 SCRATCH = {
     "own": ("sbuf", [128, CW + XW + CW], "bfloat16"),
+    "hb": ("sbuf", [128, SW], "bfloat16"),
     "rx": ("sbuf", [128, 2 * SW], "bfloat16"),
     "dg": ("sbuf", [128, SW], "bfloat16"),
     "cp": ("sbuf", [128, 4 * 3 * CW], "bfloat16"),
@@ -21,7 +22,7 @@ SCRATCH = {
     "acc3": ("psum", [128, XW], "float32"),
     "t1": ("psum", [128, XW], "float32"),
 }
-SEMAPHORES = (["ldx", "ldc1", "ldc2", "arrA", "arrB", "arrD", "sent", "va", "st"]
+SEMAPHORES = (["ldx", "ldc1", "ldc2", "harr", "arrA", "arrB", "arrD", "sent", "va", "st"]
               + ["cpo%d" % p for p in range(4)] + ["cpp%d" % p for p in range(4)] + ["fsa%d" % p for p in range(4)]
               + ["xea%d" % p for p in range(4)]
               + ["pra%d" % p for p in range(4)] + ["mm%d" % i for i in range(4)] + ["ev%d" % i for i in range(3)])
@@ -44,21 +45,63 @@ def _ring(T, topo):
     return [first, near[0], far[0], near[1]], members
 
 
+def _other_die(rc, topo, span):
+    return [c for c in range(max(0, rc - span), rc + span + 1)
+            if topo.host(c) == topo.host(rc) and topo.chip(c) == topo.chip(rc) and topo.die(c) != topo.die(rc)]
+
+
 def rank_program(g, core, T, topo):
-    me = T.rank_of(core)
-    if me is None:
-        return
     cores = list(T.cores)
     n = len(cores)
     ring, members = _ring(T, topo)
-    h = topo.host(core)
+
+    def helper_of(rc):
+        return _other_die(rc, topo, n)[members[topo.host(rc)].index(T.rank_of(rc))]
+
+    base = core
+    if T.rank_of(core) is None:
+        served = [rc for rc in cores if helper_of(rc) == core]
+        if not served:
+            return
+        base = served[0]
+    me = T.rank_of(base)
+    h = topo.host(base)
     l = members[h].index(me)
     pos = ring.index(h)
     nxt, prv, dia = ring[(pos + 1) % 4], ring[(pos - 1) % 4], ring[(pos + 2) % 4]
     rel = {h: "own", prv: "A", nxt: "B", dia: "D"}
-    even = l % 2 == 0
     S = T.sem
     peers = [q for q in range(4) if q != l]
+
+    def passes_a(q):
+        return q % 2 == 0
+
+    pass_a = passes_a(l)
+    next_first = passes_a(l)
+
+    c_nxt, c_prv = cores[members[nxt][l]], cores[members[prv][l]]
+    m_off = topo.mask(base, c_nxt) & topo.mask(base, c_prv)
+    m_on = topo.mask(base, cores[members[h][peers[0]]])
+    m_up = m_on & ~m_off
+    if _bits(m_up) not in (1, 2, 4, 8, 16):
+        m_up = m_on
+    n_off, n_on, n_up = _bits(m_off), _bits(m_on), _bits(m_up)
+    sent = [0]
+
+    def send(dst, out_ap, in_ap, sem, mask):
+        rid, pid = topo.addr(dst, core)
+        g.remote_dma(out_ap=out_ap, in_ap=in_ap, remote_sem=sem, local_sem=S.sent, pid=pid, routing_id=rid,
+                     dma_engine_mask=mask)
+        sent[0] += _bits(mask)
+
+    if base != core:
+        g.wait_ge(S.harr, n_up)
+        if next_first:
+            send(c_prv, T.rx[:, SW:2 * SW], T.hb[:, :], S.arrB, topo.mask(core, c_prv))
+        else:
+            send(c_nxt, T.rx[:, 0:SW], T.hb[:, :], S.arrA, topo.mask(core, c_nxt))
+        g.wait_ge(S.sent, sent[0])
+        return
 
     def rl(r):
         return rel[topo.host(cores[r])]
@@ -77,21 +120,6 @@ def rank_program(g, core, T, topo):
                     out.append((d, j, k))
         return out
 
-    c_nxt, c_prv = cores[members[nxt][l]], cores[members[prv][l]]
-    m_off = topo.mask(core, c_nxt) & topo.mask(core, c_prv)
-    m_on = topo.mask(core, cores[members[h][peers[0]]])
-    m_up = m_on & ~m_off
-    if _bits(m_up) not in (1, 2, 4, 8, 16):
-        m_up = m_on
-    n_off, n_on, n_up = _bits(m_off), _bits(m_on), _bits(m_up)
-    sent = [0]
-
-    def send(dst, out_ap, in_ap, sem, mask):
-        rid, pid = topo.addr(dst, core)
-        g.remote_dma(out_ap=out_ap, in_ap=in_ap, remote_sem=sem, local_sem=S.sent, pid=pid, routing_id=rid,
-                     dma_engine_mask=mask)
-        sent[0] += _bits(mask)
-
     def spread(cols, out_ap, in_ap, sem, mask):
         ids = [topo.addr(cores[members[h][q]], core) for q in cols]
         g.remote_dma_fused([RemoteDMATransfer(dst_ids=[DstId(rid=a[0], pnc=a[1]) for a in ids], dma_engine_mask=mask,
@@ -100,23 +128,28 @@ def rank_program(g, core, T, topo):
         sent[0] += _bits(mask)
 
     c_lo, c_hi = T.own[:, 0:CW], T.own[:, CW + XW:CW + XW + CW]
-    c_1st, c_2nd = (c_hi, c_lo) if even else (c_lo, c_hi)
-    t_a, t_b = (3.0, 4.0) if even else (4.0, 3.0)
+    c_1st, c_2nd = (c_hi, c_lo) if next_first else (c_lo, c_hi)
+    t_a, t_b = (3.0, 5.0) if pass_a else (5.0, 3.0)
+
+    def far_at(q):
+        return (0, XW) if passes_a(q) else (CW, 0)
+
+    fx, fc = far_at(l)
 
     def xloc(j):
         r_, q = rl(j), col(j)
         if q != l:
             if r_ == "D":
-                b = q * SW + (0 if q % 2 == 0 else CW)
+                b = q * SW + far_at(q)[0]
                 return T.fs[:, b:b + XW], ("fsa%d" % q, n_on), 9.5
-            return T.xe[:, q * XW:(q + 1) * XW], ("xea%d" % q, n_on), 8.0
+            return T.xe[:, q * XW:(q + 1) * XW], ("xea%d" % q, n_up if r_ == "own" else n_on), 8.0
         if r_ == "own":
             return T.own[:, CW:CW + XW], ("ldx", 16), 0.0
         if r_ == "A":
             return T.rx[:, 0:XW], ("arrA", n_off), t_a
         if r_ == "B":
             return T.rx[:, SW + CW:2 * SW], ("arrB", n_off), t_b
-        return (T.dg[:, 0:XW] if even else T.dg[:, CW:SW]), ("arrD", n_off), 6.5
+        return T.dg[:, fx:fx + XW], ("arrD", n_off), 6.5
 
     def cloc(k):
         r_, q = rl(k), col(k)
@@ -127,9 +160,9 @@ def rank_program(g, core, T, topo):
                 return T.rx[:, XW:SW], ("arrA", n_off), t_a
             if r_ == "B":
                 return T.rx[:, SW:SW + CW], ("arrB", n_off), t_b
-            return (T.dg[:, XW:SW] if even else T.dg[:, 0:CW]), ("arrD", n_off), 6.5
+            return T.dg[:, fc:fc + CW], ("arrD", n_off), 6.5
         if r_ == "D":
-            b = q * SW + (XW if q % 2 == 0 else 0)
+            b = q * SW + far_at(q)[1]
             return T.fs[:, b:b + CW], ("fsa%d" % q, n_on), 9.5
         b = q * 3 * CW
         if r_ == "own":
@@ -154,40 +187,35 @@ def rank_program(g, core, T, topo):
     g.scalar.dma_start(c_1st, T.c[:, :]).then_inc(S.ldc1, 16)
     g.scalar.dma_start(c_2nd, T.c[:, :]).then_inc(S.ldc2, 16)
 
-    def send_next():
-        send(c_nxt, T.rx[:, 0:SW], T.own[:, CW:CW + SW], S.arrA, m_off)
-
-    def send_prev():
-        send(c_prv, T.rx[:, SW:2 * SW], T.own[:, 0:SW], S.arrB, m_off)
-
-    def near_x(which):
+    def near_x(own_x, mask):
         for j in sorted(need_x):
-            if need_x[j] and (rl(j) == "own") == which:
-                spread(need_x[j], T.xe[:, l * XW:(l + 1) * XW], xloc(j)[0], S["xea%d" % l], m_on)
+            if need_x[j] and (rl(j) == "own") == own_x:
+                spread(need_x[j], T.xe[:, l * XW:(l + 1) * XW], xloc(j)[0], S["xea%d" % l], mask)
 
+    hc = helper_of(core)
     g.wait_ge(S.ldc1, 16)
     g.wait_ge(S.ldx, 16)
-    if even:
-        send_next()
+    if next_first:
+        send(c_nxt, T.rx[:, 0:SW], T.own[:, CW:CW + SW], S.arrA, m_off)
         g.wait_ge(S.ldc2, 16)
-        send_prev()
+        send(hc, T.hb[:, :], T.own[:, 0:SW], S.harr, m_up)
     else:
-        send_prev()
+        send(c_prv, T.rx[:, SW:2 * SW], T.own[:, 0:SW], S.arrB, m_off)
         g.wait_ge(S.ldc2, 16)
-        send_next()
+        send(hc, T.hb[:, :], T.own[:, CW:CW + SW], S.harr, m_up)
     if need_o:
         spread(need_o, T.cp[:, l * 3 * CW:l * 3 * CW + CW], c_1st, S["cpo%d" % l], m_up)
-    if even:
+    near_x(True, m_up)
+    if pass_a:
         g.wait_ge(S.arrA, n_off)
         send(c_nxt, T.dg[:, :], T.rx[:, 0:SW], S.arrD, m_off)
     else:
         g.wait_ge(S.arrB, n_off)
         send(c_prv, T.dg[:, :], T.rx[:, SW:2 * SW], S.arrD, m_off)
-    g.wait_ge(S.arrB if even else S.arrA, n_off)
+    g.wait_ge(S.arrB if pass_a else S.arrA, n_off)
     if need_p:
         spread(need_p, T.cp[:, l * 3 * CW + CW:l * 3 * CW + 3 * CW], T.rx[:, XW:XW + 2 * CW], S["cpp%d" % l], m_on)
-    near_x(True)
-    near_x(False)
+    near_x(False, m_on)
     g.wait_ge(S.arrD, n_off)
     spread(peers, T.fs[:, l * SW:(l + 1) * SW], T.dg[:, :], S["fsa%d" % l], m_on)
 

from concourse.bass import DstId, RemoteDMATransfer
from concourse.mybir import AluOpType

CW, XW = 128, 512
SW = CW + XW

SCRATCH = {
    "own": ("sbuf", [128, CW + XW + CW], "bfloat16"),
    "hb": ("sbuf", [128, SW], "bfloat16"),
    "rx": ("sbuf", [128, 2 * SW], "bfloat16"),
    "dg": ("sbuf", [128, SW], "bfloat16"),
    "cp": ("sbuf", [128, 4 * 3 * CW], "bfloat16"),
    "fs": ("sbuf", [128, 4 * SW], "bfloat16"),
    "xe": ("sbuf", [128, 4 * XW], "bfloat16"),
    "pb": ("sbuf", [128, 3 * XW], "bfloat16"),
    "pr": ("sbuf", [128, 4 * XW], "bfloat16"),
    "e1": ("sbuf", [128, XW], "float32"),
    "ysb": ("sbuf", [128, XW], "bfloat16"),
    "acc0": ("psum", [128, XW], "float32"),
    "acc1": ("psum", [128, XW], "float32"),
    "acc2": ("psum", [128, XW], "float32"),
    "acc3": ("psum", [128, XW], "float32"),
    "t1": ("psum", [128, XW], "float32"),
}
SEMAPHORES = (["ldx", "ldc1", "ldc2", "harr", "arrA", "arrB", "arrD", "sent", "va", "st"]
              + ["cpo%d" % p for p in range(4)] + ["cpp%d" % p for p in range(4)] + ["fsa%d" % p for p in range(4)]
              + ["xea%d" % p for p in range(4)]
              + ["pra%d" % p for p in range(4)] + ["mm%d" % i for i in range(4)] + ["ev%d" % i for i in range(3)])


def _bits(mask):
    return bin(mask).count("1")


def _ring(T, topo):
    cores = list(T.cores)
    hosts = []
    for c in cores:
        if topo.host(c) not in hosts:
            hosts.append(topo.host(c))
    members = {h: [r for r, c in enumerate(cores) if topo.host(c) == h] for h in hosts}
    first = hosts[0]
    near = [h for h in hosts[1:] if topo.may_write(cores[members[first][0]], cores[members[h][0]])]
    far = [h for h in hosts[1:] if h not in near]
    return [first, near[0], far[0], near[1]], members


def _other_die(rc, topo, span):
    return [c for c in range(max(0, rc - span), rc + span + 1)
            if topo.host(c) == topo.host(rc) and topo.chip(c) == topo.chip(rc) and topo.die(c) != topo.die(rc)]


def rank_program(g, core, T, topo):
    cores = list(T.cores)
    n = len(cores)
    ring, members = _ring(T, topo)

    def helper_of(rc):
        return _other_die(rc, topo, n)[members[topo.host(rc)].index(T.rank_of(rc))]

    base = core
    if T.rank_of(core) is None:
        served = [rc for rc in cores if helper_of(rc) == core]
        if not served:
            return
        base = served[0]
    me = T.rank_of(base)
    h = topo.host(base)
    l = members[h].index(me)
    pos = ring.index(h)
    nxt, prv, dia = ring[(pos + 1) % 4], ring[(pos - 1) % 4], ring[(pos + 2) % 4]
    rel = {h: "own", prv: "A", nxt: "B", dia: "D"}
    S = T.sem
    peers = [q for q in range(4) if q != l]

    def passes_a(q):
        return q % 2 == 0

    pass_a = passes_a(l)
    next_first = passes_a(l)

    c_nxt, c_prv = cores[members[nxt][l]], cores[members[prv][l]]
    m_off = topo.mask(base, c_nxt) & topo.mask(base, c_prv)
    m_on = topo.mask(base, cores[members[h][peers[0]]])
    m_up = m_on & ~m_off
    if _bits(m_up) not in (1, 2, 4, 8, 16):
        m_up = m_on
    n_off, n_on, n_up = _bits(m_off), _bits(m_on), _bits(m_up)
    sent = [0]

    def send(dst, out_ap, in_ap, sem, mask):
        rid, pid = topo.addr(dst, core)
        g.remote_dma(out_ap=out_ap, in_ap=in_ap, remote_sem=sem, local_sem=S.sent, pid=pid, routing_id=rid,
                     dma_engine_mask=mask)
        sent[0] += _bits(mask)

    if base != core:
        g.wait_ge(S.harr, n_up)
        if next_first:
            send(c_prv, T.rx[:, SW:2 * SW], T.hb[:, :], S.arrB, topo.mask(core, c_prv))
        else:
            send(c_nxt, T.rx[:, 0:SW], T.hb[:, :], S.arrA, topo.mask(core, c_nxt))
        g.wait_ge(S.sent, sent[0])
        return

    def rl(r):
        return rel[topo.host(cores[r])]

    def col(r):
        return members[topo.host(cores[r])].index(r)

    def prods_of(lp):
        out = []
        for d in range(4):
            r = members[h][d]
            for j in range(n):
                k = (r - j) % n
                late = rl(j) == "D" or rl(k) == "D"
                if (late and d == lp) or (not late and col(j) == lp):
                    out.append((d, j, k))
        return out

    def spread(cols, out_ap, in_ap, sem, mask):
        ids = [topo.addr(cores[members[h][q]], core) for q in cols]
        g.remote_dma_fused([RemoteDMATransfer(dst_ids=[DstId(rid=a[0], pnc=a[1]) for a in ids], dma_engine_mask=mask,
                                              remote_sem=sem, srcs=[in_ap], dsts=[out_ap for a in ids], alu_op=0)],
                           local_sem=S.sent)
        sent[0] += _bits(mask)

    c_lo, c_hi = T.own[:, 0:CW], T.own[:, CW + XW:CW + XW + CW]
    c_1st, c_2nd = (c_hi, c_lo) if next_first else (c_lo, c_hi)
    t_a, t_b = (3.0, 5.0) if pass_a else (5.0, 3.0)

    def far_at(q):
        return (0, XW) if passes_a(q) else (CW, 0)

    fx, fc = far_at(l)

    def xloc(j):
        r_, q = rl(j), col(j)
        if q != l:
            if r_ == "D":
                b = q * SW + far_at(q)[0]
                return T.fs[:, b:b + XW], ("fsa%d" % q, n_on), 9.5
            return T.xe[:, q * XW:(q + 1) * XW], ("xea%d" % q, n_up if r_ == "own" else n_on), 8.0
        if r_ == "own":
            return T.own[:, CW:CW + XW], ("ldx", 16), 0.0
        if r_ == "A":
            return T.rx[:, 0:XW], ("arrA", n_off), t_a
        if r_ == "B":
            return T.rx[:, SW + CW:2 * SW], ("arrB", n_off), t_b
        return T.dg[:, fx:fx + XW], ("arrD", n_off), 6.5

    def cloc(k):
        r_, q = rl(k), col(k)
        if q == l:
            if r_ == "own":
                return c_1st, ("ldc1", 16), 0.0
            if r_ == "A":
                return T.rx[:, XW:SW], ("arrA", n_off), t_a
            if r_ == "B":
                return T.rx[:, SW:SW + CW], ("arrB", n_off), t_b
            return T.dg[:, fc:fc + CW], ("arrD", n_off), 6.5
        if r_ == "D":
            b = q * SW + far_at(q)[1]
            return T.fs[:, b:b + CW], ("fsa%d" % q, n_on), 9.5
        b = q * 3 * CW
        if r_ == "own":
            return T.cp[:, b:b + CW], ("cpo%d" % q, n_up), 4.5
        if r_ == "A":
            return T.cp[:, b + CW:b + 2 * CW], ("cpp%d" % q, n_on), 7.0
        return T.cp[:, b + 2 * CW:b + 3 * CW], ("cpp%d" % q, n_on), 7.0

    need_o, need_p, need_x = [], [], {}
    for q in peers:
        pq = prods_of(q)
        ks = [k for (_, _, k) in pq if col(k) == l]
        if any(rl(k) == "own" for k in ks):
            need_o.append(q)
        if any(rl(k) in ("A", "B") for k in ks):
            need_p.append(q)
        for (_, j, _) in pq:
            if col(j) == l and rl(j) != "D" and q not in need_x.setdefault(j, []):
                need_x[j].append(q)

    g.sync.dma_start(T.own[:, CW:CW + XW], T.x[:, :]).then_inc(S.ldx, 16)
    g.scalar.dma_start(c_1st, T.c[:, :]).then_inc(S.ldc1, 16)
    g.scalar.dma_start(c_2nd, T.c[:, :]).then_inc(S.ldc2, 16)

    def near_x(own_x, mask):
        for j in sorted(need_x):
            if need_x[j] and (rl(j) == "own") == own_x:
                spread(need_x[j], T.xe[:, l * XW:(l + 1) * XW], xloc(j)[0], S["xea%d" % l], mask)

    hc = helper_of(core)
    g.wait_ge(S.ldc1, 16)
    g.wait_ge(S.ldx, 16)
    if next_first:
        send(c_nxt, T.rx[:, 0:SW], T.own[:, CW:CW + SW], S.arrA, m_off)
        g.wait_ge(S.ldc2, 16)
        send(hc, T.hb[:, :], T.own[:, 0:SW], S.harr, m_up)
    else:
        send(c_prv, T.rx[:, SW:2 * SW], T.own[:, 0:SW], S.arrB, m_off)
        g.wait_ge(S.ldc2, 16)
        send(hc, T.hb[:, :], T.own[:, CW:CW + SW], S.harr, m_up)
    if need_o:
        spread(need_o, T.cp[:, l * 3 * CW:l * 3 * CW + CW], c_1st, S["cpo%d" % l], m_up)
    near_x(True, m_up)
    if pass_a:
        g.wait_ge(S.arrA, n_off)
        send(c_nxt, T.dg[:, :], T.rx[:, 0:SW], S.arrD, m_off)
    else:
        g.wait_ge(S.arrB, n_off)
        send(c_prv, T.dg[:, :], T.rx[:, SW:2 * SW], S.arrD, m_off)
    g.wait_ge(S.arrB if pass_a else S.arrA, n_off)
    if need_p:
        spread(need_p, T.cp[:, l * 3 * CW + CW:l * 3 * CW + 3 * CW], T.rx[:, XW:XW + 2 * CW], S["cpp%d" % l], m_on)
    near_x(False, m_on)
    g.wait_ge(S.arrD, n_off)
    spread(peers, T.fs[:, l * SW:(l + 1) * SW], T.dg[:, :], S["fsa%d" % l], m_on)

    items = []
    for (d, j, k) in prods_of(l):
        xa, xs, xt = xloc(j)
        ca, cs, ct = cloc(k)
        items.append((max(xt, ct), (d - l - 1) % 4, d, xa, xs, ca, cs))
    items.sort(key=lambda t: (t[0], t[1]))
    mine = [t for t in items if t[2] == l]
    oth = [t for t in items if t[2] != l]
    last = {}
    for t in oth:
        last[t[2]] = t
    tail = sorted(last.values(), key=lambda t: t[1])
    oth = [t for t in oth if last[t[2]] is not t] + tail
    seq = [t for t in mine if t[0] <= 4.5] + oth + [t for t in mine if t[0] > 4.5]
    total = [0, 0, 0, 0]
    for t in seq:
        total[t[2]] += 1

    acc = [T.acc0, T.acc1, T.acc2, T.acc3]
    seen, done, order = set(), [0, 0, 0, 0], []
    for (_, _, d, xa, xs, ca, cs) in seq:
        for sm in (xs, cs):
            if sm not in seen:
                seen.add(sm)
                g.tensor.wait_ge(S[sm[0]], sm[1])
        done[d] += 1
        mmi = g.tensor.matmul(out=acc[d][:, :], lhsT=ca, rhs=xa, start=done[d] == 1, stop=done[d] == total[d])
        if done[d] == total[d]:
            mmi.then_inc(S["mm%d" % d], 1)
            if d != l:
                order.append(d)

    for i, d in enumerate(order):
        g.vector.wait_ge(S["mm%d" % d], 1)
        g.vector.tensor_copy(out=T.pb[:, i * XW:(i + 1) * XW], in_=acc[d][:, :]).then_inc(S["ev%d" % i], 1)
        g.wait_ge(S["ev%d" % i], 1)
        send(cores[members[h][d]], T.pr[:, l * XW:(l + 1) * XW], T.pb[:, i * XW:(i + 1) * XW], S["pra%d" % l], m_on)

    q1, q2, q3 = (l - 1) % 4, (l - 2) % 4, (l - 3) % 4
    g.vector.wait_ge(S["pra%d" % q1], n_on)
    g.vector.wait_ge(S["pra%d" % q2], n_on)
    g.vector.tensor_tensor(out=T.e1[:, :], in0=T.pr[:, q1 * XW:(q1 + 1) * XW], in1=T.pr[:, q2 * XW:(q2 + 1) * XW],
                           op=AluOpType.add).then_inc(S.va, 1)
    g.vector.wait_ge(S.va, 1)
    g.vector.wait_ge(S["mm%d" % l], 1)
    g.vector.tensor_tensor(out=T.t1[:, :], in0=acc[l][:, :], in1=T.e1[:, :], op=AluOpType.add).then_inc(S.va, 1)
    g.vector.wait_ge(S.va, 2)
    g.vector.wait_ge(S["pra%d" % q3], n_on)
    g.vector.tensor_tensor(out=T.ysb[:, :], in0=T.t1[:, :], in1=T.pr[:, q3 * XW:(q3 + 1) * XW],
                           op=AluOpType.add).then_inc(S.va, 1)
    g.sync.wait_ge(S.va, 3)
    g.sync.dma_start(T.y[:, :], T.ysb[:, :]).then_inc(S.st, 16)
    g.wait_ge(S.sent, sent[0])
    g.wait_ge(S.st, 16)
